import numpy as np
CORES = [3,11,19,27,35,43,51,59,67,75,83,91,99,107,115,123,131,139,147,155,163,171,179,187,195,203,211,219,227,235,243,251]
N = 32
def setup_inputs(rng):
    return {"x": rng.standard_normal((N, 128, 1024), dtype=np.float32)}
def reference(x):
    s = x.sum(axis=0, dtype=np.float64).astype(x.dtype)
    b = 1024 // N
    return {"y": np.stack([s[:, r * b:(r + 1) * b] for r in range(N)])}

@@ -1,0 +1,198 @@
+from concourse.bass import RemoteDMATransfer, DstId
+from concourse.mybir import AluOpType
+
+NR = 32
+BW = 32
+PHASES = [[4, 3, 2, 1, 0]]
+HOLD = [3, 2]
+SOLO = [False]
+CHUNK = False
+RELAY = []
+NP = len(PHASES)
+
+
+def used(p):
+    return [b for ph in PHASES[:p] for b in ph]
+
+
+def dests(c, p):
+    m = sum(1 << b for b in used(p))
+    return [r for r in range(NR) if (r & m) == (c & m)]
+
+
+def group(c, p):
+    m = sum(1 << b for b in PHASES[p])
+    return [t for t in range(NR) if (t & ~m) == (c & ~m)]
+
+
+def width(p):
+    return BW * (NR >> len(used(p)))
+
+
+def pow2floor(n):
+    e = 1
+    while e * 2 <= n:
+        e *= 2
+    return e
+
+
+def phase_calls(c, p):
+    dc = dests(c, p)
+    grp = group(c, p)
+    g = len(grp)
+    slot = grp.index(c)
+    wn = width(p + 1)
+    off, on = [], []
+    for j in range(g):
+        t = grp[(slot + j) % g]
+        pos = [dc.index(r) for r in dests(t, p + 1)]
+        o = 0
+        while o < len(pos):
+            n = 1
+            while o + n < len(pos) and pos[o + n] == pos[o] + n:
+                n += 1
+            (on if t == c else off).append((t, pos[o] * BW, slot * wn + o * BW, n * BW))
+            o += n
+    calls = []
+    if SOLO[p]:
+        for tr in off:
+            calls.append([(tr[0], 0x00FF) + tr[1:]])
+        e = pow2floor(8 // len(on))
+        calls[-1] = calls[-1] + [(tr[0], ((1 << e) - 1) << (8 + i * e)) + tr[1:] for i, tr in enumerate(on)]
+        return calls
+    nc = (len(off) + 7) // 8
+    for q in range(nc):
+        a = off[q::nc]
+        b = on[q::nc]
+        e = pow2floor(8 // len(a))
+        call = [(tr[0], ((1 << e) - 1) << (i * e)) + tr[1:] for i, tr in enumerate(a)]
+        if b:
+            e = pow2floor(8 // len(b))
+            call += [(tr[0], ((1 << e) - 1) << (8 + i * e)) + tr[1:] for i, tr in enumerate(b)]
+        calls.append(call)
+    return calls
+
+
+def bits(m):
+    return bin(m).count("1")
+
+
+def arrivals(t, p, own):
+    return sum(bits(tr[1]) for c in group(t, p) for call in phase_calls(c, p) for tr in call
+               if tr[0] == t and (c == t) == own)
+
+
+LOCAL_END = HOLD[NP] == 3
+NLOAD = (len(phase_calls(0, 0)) + 1) if CHUNK else 1
+SCRATCH = {"xs": ("sbuf", [128, NR * BW], "float32"), "fin": ("sbuf", [128, BW], "float32")}
+for ph in range(NP):
+    SCRATCH["L%d" % ph] = ("sbuf", [128, (1 << len(PHASES[ph])) * width(ph + 1)], "float32")
+SEMAPHORES = ["st", "sent", "af", "own", "rl"] + ["a%d" % ph for ph in range(NP)] + ["ld%d" % i for i in range(NLOAD)]
+
+
+def land_of(T, p):
+    return [T.L0, T.L1 if NP > 1 else None, T.L2 if NP > 2 else None, T.L3 if NP > 3 else None,
+            T.L4 if NP > 4 else None][p]
+
+
+def sem(T, p):
+    return [T.sem.a0, T.sem.a1 if NP > 1 else None, T.sem.a2 if NP > 2 else None, T.sem.a3 if NP > 3 else None,
+            T.sem.a4 if NP > 4 else None][p]
+
+
+def ldsem(T, i):
+    return [T.sem.ld0, T.sem.ld1 if NLOAD > 1 else None, T.sem.ld2 if NLOAD > 2 else None,
+            T.sem.ld3 if NLOAD > 3 else None, T.sem.ld4 if NLOAD > 4 else None, T.sem.ld5 if NLOAD > 5 else None,
+            T.sem.ld6 if NLOAD > 6 else None, T.sem.ld7 if NLOAD > 7 else None, T.sem.ld8 if NLOAD > 8 else None][i]
+
+
+def emit(g, core, T, topo, p, call, src, ns, w):
+    c = core // 8
+    trs, n_sent = [], 0
+    for (t, m, a, b, n) in call:
+        rid, pid = topo.addr(8 * t + HOLD[p + 1], core)
+        rs = T.sem.own if (LOCAL_END and p == NP - 1 and t == c) else sem(T, p)
+        trs.append(RemoteDMATransfer(dst_ids=[DstId(rid=rid, pnc=pid)], dma_engine_mask=m, remote_sem=rs,
+                                     srcs=[src[:, s * w + a:s * w + a + n] for s in range(ns)],
+                                     dsts=[land_of(T, p)[:, b:b + n]], alu_op=1 if ns > 1 else 0))
+        n_sent += bits(m)
+    g.remote_dma_fused(trs, local_sem=T.sem.sent)
+    return n_sent
+
+
+def rank_program(g, core, T, topo):
+    c, l = core // 8, core % 8
+    if l not in HOLD and l not in RELAY:
+        return
+    sent = 0
+    calls0 = phase_calls(c, 0)
+    relay = RELAY if RELAY else [3] * len(calls0)
+    if l != 3 and l in relay:
+        mine = [i for i in range(len(calls0)) if relay[i] == l]
+        g.wait_ge(T.sem.rl, 8 * len(mine))
+        for i in mine:
+            sent += emit(g, core, T, topo, 0, calls0[i], T.xs, 1, NR * BW)
+    for p in range(NP + 1):
+        if HOLD[p] != l:
+            continue
+        if p == 0:
+            order = [i for i in range(len(calls0)) if relay[i] != 3] + [i for i in range(len(calls0)) if relay[i] == 3]
+            if CHUNK:
+                for k, i in enumerate(order):
+                    for (t, m, a, b, n) in calls0[i]:
+                        if t != c:
+                            g.dma_start(T.xs[:, a:a + n], T.x[:, a:a + n]).then_inc(ldsem(T, k), 16)
+                for (t, m, a, b, n) in calls0[-1]:
+                    if t == c:
+                        g.dma_start(T.xs[:, a:a + n], T.x[:, a:a + n]).then_inc(ldsem(T, NLOAD - 1), 16)
+            else:
+                g.dma_start(T.xs[:], T.x[:]).then_inc(T.sem.ld0, 16)
+                g.wait_ge(T.sem.ld0, 16)
+            for k, i in enumerate(order):
+                call = calls0[i]
+                if CHUNK:
+                    g.wait_ge(ldsem(T, k), 16)
+                    if i == len(calls0) - 1:
+                        g.wait_ge(ldsem(T, NLOAD - 1), 16)
+                if relay[i] == 3:
+                    sent += emit(g, core, T, topo, 0, call, T.xs, 1, NR * BW)
+                else:
+                    keep = [tr for tr in call if tr[0] == c]
+                    (t, m, a, b, n) = [tr for tr in call if tr[0] != c][0]
+                    rid, pid = topo.addr(8 * c + relay[i], core)
+                    g.remote_dma(T.xs[:, a:a + n], T.xs[:, a:a + n], T.sem.rl, T.sem.sent, pid, rid, 0xFF00)
+                    sent += 8
+                    assert not keep
+            continue
+        if not (LOCAL_END and p == NP):
+            g.wait_ge(sem(T, p - 1), arrivals(c, p - 1, False) + arrivals(c, p - 1, True))
+        src, ns, w = land_of(T, p - 1), 1 << len(PHASES[p - 1]), width(p)
+        if p < NP:
+            for call in phase_calls(c, p):
+                sent += emit(g, core, T, topo, p, call, src, ns, w)
+        elif not LOCAL_END:
+            rid, pid = topo.addr(8 * c + 3, core)
+            g.remote_dma_fused([RemoteDMATransfer(dst_ids=[DstId(rid=rid, pnc=pid)], dma_engine_mask=0xFFFF,
+                                                  remote_sem=T.sem.af,
+                                                  srcs=[src[:, s * BW:(s + 1) * BW] for s in range(ns)],
+                                                  dsts=[T.fin[:]], alu_op=1)], local_sem=T.sem.sent)
+            sent += 16
+    if l == 3:
+        if LOCAL_END:
+            src, grp = land_of(T, NP - 1), group(c, NP - 1)
+            me = grp.index(c)
+            g.wait_ge(T.sem.own, arrivals(c, NP - 1, True))
+            g.dma_start(T.y[:], src[:, me * BW:(me + 1) * BW]).then_inc(T.sem.st, 16)
+            g.wait_ge(sem(T, NP - 1), arrivals(c, NP - 1, False))
+            k = 16
+            for s in range(len(grp)):
+                if s != me:
+                    g.wait_ge(T.sem.st, k)
+                    g.dma_start(T.y[:], src[:, s * BW:(s + 1) * BW], accum_op=AluOpType.add).then_inc(T.sem.st, 16)
+                    k += 16
+            g.wait_ge(T.sem.st, k)
+        else:
+            g.wait_ge(T.sem.af, 16)
+            g.dma_start(T.y[:], T.fin[:]).then_inc(T.sem.st, 16)
+            g.wait_ge(T.sem.st, 16)
+    g.wait_ge(T.sem.sent, sent)

@@ -1,198 +1,68 @@
 from concourse.bass import RemoteDMATransfer, DstId
-from concourse.mybir import AluOpType
 
 NR = 32
 BW = 32
-PHASES = [[4, 3, 2, 1, 0]]
-HOLD = [3, 2]
-SOLO = [False]
-CHUNK = False
-RELAY = []
-NP = len(PHASES)
+QW = 256
+COL = 1
+HELP = [7, 6, 2]
+
+SCRATCH = {
+    "xs": ("sbuf", [128, NR * BW], "float32"),
+    "rq": ("sbuf", [128, QW], "float32"),
+    "land": ("sbuf", [128, NR * BW], "float32"),
+    "fin": ("sbuf", [128, BW], "float32"),
+}
+SEMAPHORES = ["ld0", "ld1", "ld2", "ld3", "st", "sent", "rl", "arr", "af"]
 
 
-def used(p):
-    return [b for ph in PHASES[:p] for b in ph]
+def quarter(c, l):
+    return (c >> 3) ^ {3: 0, 2: 1, 7: 2, 6: 3}[l]
 
 
-def dests(c, p):
-    m = sum(1 << b for b in used(p))
-    return [r for r in range(NR) if (r & m) == (c & m)]
-
-
-def group(c, p):
-    m = sum(1 << b for b in PHASES[p])
-    return [t for t in range(NR) if (t & ~m) == (c & ~m)]
-
-
-def width(p):
-    return BW * (NR >> len(used(p)))
-
-
-def pow2floor(n):
-    e = 1
-    while e * 2 <= n:
-        e *= 2
-    return e
-
-
-def phase_calls(c, p):
-    dc = dests(c, p)
-    grp = group(c, p)
-    g = len(grp)
-    slot = grp.index(c)
-    wn = width(p + 1)
-    off, on = [], []
-    for j in range(g):
-        t = grp[(slot + j) % g]
-        pos = [dc.index(r) for r in dests(t, p + 1)]
-        o = 0
-        while o < len(pos):
-            n = 1
-            while o + n < len(pos) and pos[o + n] == pos[o] + n:
-                n += 1
-            (on if t == c else off).append((t, pos[o] * BW, slot * wn + o * BW, n * BW))
-            o += n
-    calls = []
-    if SOLO[p]:
-        for tr in off:
-            calls.append([(tr[0], 0x00FF) + tr[1:]])
-        e = pow2floor(8 // len(on))
-        calls[-1] = calls[-1] + [(tr[0], ((1 << e) - 1) << (8 + i * e)) + tr[1:] for i, tr in enumerate(on)]
-        return calls
-    nc = (len(off) + 7) // 8
-    for q in range(nc):
-        a = off[q::nc]
-        b = on[q::nc]
-        e = pow2floor(8 // len(a))
-        call = [(tr[0], ((1 << e) - 1) << (i * e)) + tr[1:] for i, tr in enumerate(a)]
-        if b:
-            e = pow2floor(8 // len(b))
-            call += [(tr[0], ((1 << e) - 1) << (8 + i * e)) + tr[1:] for i, tr in enumerate(b)]
-        calls.append(call)
-    return calls
-
-
-def bits(m):
-    return bin(m).count("1")
-
-
-def arrivals(t, p, own):
-    return sum(bits(tr[1]) for c in group(t, p) for call in phase_calls(c, p) for tr in call
-               if tr[0] == t and (c == t) == own)
-
-
-LOCAL_END = HOLD[NP] == 3
-NLOAD = (len(phase_calls(0, 0)) + 1) if CHUNK else 1
-SCRATCH = {"xs": ("sbuf", [128, NR * BW], "float32"), "fin": ("sbuf", [128, BW], "float32")}
-for ph in range(NP):
-    SCRATCH["L%d" % ph] = ("sbuf", [128, (1 << len(PHASES[ph])) * width(ph + 1)], "float32")
-SEMAPHORES = ["st", "sent", "af", "own", "rl"] + ["a%d" % ph for ph in range(NP)] + ["ld%d" % i for i in range(NLOAD)]
-
-
-def land_of(T, p):
-    return [T.L0, T.L1 if NP > 1 else None, T.L2 if NP > 2 else None, T.L3 if NP > 3 else None,
-            T.L4 if NP > 4 else None][p]
-
-
-def sem(T, p):
-    return [T.sem.a0, T.sem.a1 if NP > 1 else None, T.sem.a2 if NP > 2 else None, T.sem.a3 if NP > 3 else None,
-            T.sem.a4 if NP > 4 else None][p]
-
-
-def ldsem(T, i):
-    return [T.sem.ld0, T.sem.ld1 if NLOAD > 1 else None, T.sem.ld2 if NLOAD > 2 else None,
-            T.sem.ld3 if NLOAD > 3 else None, T.sem.ld4 if NLOAD > 4 else None, T.sem.ld5 if NLOAD > 5 else None,
-            T.sem.ld6 if NLOAD > 6 else None, T.sem.ld7 if NLOAD > 7 else None, T.sem.ld8 if NLOAD > 8 else None][i]
-
-
-def emit(g, core, T, topo, p, call, src, ns, w):
+def send(g, core, T, topo, src, base, q):
     c = core // 8
-    trs, n_sent = [], 0
-    for (t, m, a, b, n) in call:
-        rid, pid = topo.addr(8 * t + HOLD[p + 1], core)
-        rs = T.sem.own if (LOCAL_END and p == NP - 1 and t == c) else sem(T, p)
-        trs.append(RemoteDMATransfer(dst_ids=[DstId(rid=rid, pnc=pid)], dma_engine_mask=m, remote_sem=rs,
-                                     srcs=[src[:, s * w + a:s * w + a + n] for s in range(ns)],
-                                     dsts=[land_of(T, p)[:, b:b + n]], alu_op=1 if ns > 1 else 0))
-        n_sent += bits(m)
+    trs = []
+    for i in range(8):
+        k = (i + c) % 8
+        rid, pid = topo.addr(8 * (8 * q + k) + COL, core)
+        trs.append(RemoteDMATransfer(dst_ids=[DstId(rid=rid, pnc=pid)], dma_engine_mask=1 << i, remote_sem=T.sem.arr,
+                                     src=src[:, base + k * BW:base + (k + 1) * BW],
+                                     dst=T.land[:, c * BW:(c + 1) * BW]))
     g.remote_dma_fused(trs, local_sem=T.sem.sent)
-    return n_sent
+    return 8
 
 
 def rank_program(g, core, T, topo):
     c, l = core // 8, core % 8
-    if l not in HOLD and l not in RELAY:
-        return
-    sent = 0
-    calls0 = phase_calls(c, 0)
-    relay = RELAY if RELAY else [3] * len(calls0)
-    if l != 3 and l in relay:
-        mine = [i for i in range(len(calls0)) if relay[i] == l]
-        g.wait_ge(T.sem.rl, 8 * len(mine))
-        for i in mine:
-            sent += emit(g, core, T, topo, 0, calls0[i], T.xs, 1, NR * BW)
-    for p in range(NP + 1):
-        if HOLD[p] != l:
-            continue
-        if p == 0:
-            order = [i for i in range(len(calls0)) if relay[i] != 3] + [i for i in range(len(calls0)) if relay[i] == 3]
-            if CHUNK:
-                for k, i in enumerate(order):
-                    for (t, m, a, b, n) in calls0[i]:
-                        if t != c:
-                            g.dma_start(T.xs[:, a:a + n], T.x[:, a:a + n]).then_inc(ldsem(T, k), 16)
-                for (t, m, a, b, n) in calls0[-1]:
-                    if t == c:
-                        g.dma_start(T.xs[:, a:a + n], T.x[:, a:a + n]).then_inc(ldsem(T, NLOAD - 1), 16)
-            else:
-                g.dma_start(T.xs[:], T.x[:]).then_inc(T.sem.ld0, 16)
-                g.wait_ge(T.sem.ld0, 16)
-            for k, i in enumerate(order):
-                call = calls0[i]
-                if CHUNK:
-                    g.wait_ge(ldsem(T, k), 16)
-                    if i == len(calls0) - 1:
-                        g.wait_ge(ldsem(T, NLOAD - 1), 16)
-                if relay[i] == 3:
-                    sent += emit(g, core, T, topo, 0, call, T.xs, 1, NR * BW)
-                else:
-                    keep = [tr for tr in call if tr[0] == c]
-                    (t, m, a, b, n) = [tr for tr in call if tr[0] != c][0]
-                    rid, pid = topo.addr(8 * c + relay[i], core)
-                    g.remote_dma(T.xs[:, a:a + n], T.xs[:, a:a + n], T.sem.rl, T.sem.sent, pid, rid, 0xFF00)
-                    sent += 8
-                    assert not keep
-            continue
-        if not (LOCAL_END and p == NP):
-            g.wait_ge(sem(T, p - 1), arrivals(c, p - 1, False) + arrivals(c, p - 1, True))
-        src, ns, w = land_of(T, p - 1), 1 << len(PHASES[p - 1]), width(p)
-        if p < NP:
-            for call in phase_calls(c, p):
-                sent += emit(g, core, T, topo, p, call, src, ns, w)
-        elif not LOCAL_END:
-            rid, pid = topo.addr(8 * c + 3, core)
-            g.remote_dma_fused([RemoteDMATransfer(dst_ids=[DstId(rid=rid, pnc=pid)], dma_engine_mask=0xFFFF,
-                                                  remote_sem=T.sem.af,
-                                                  srcs=[src[:, s * BW:(s + 1) * BW] for s in range(ns)],
-                                                  dsts=[T.fin[:]], alu_op=1)], local_sem=T.sem.sent)
-            sent += 16
     if l == 3:
-        if LOCAL_END:
-            src, grp = land_of(T, NP - 1), group(c, NP - 1)
-            me = grp.index(c)
-            g.wait_ge(T.sem.own, arrivals(c, NP - 1, True))
-            g.dma_start(T.y[:], src[:, me * BW:(me + 1) * BW]).then_inc(T.sem.st, 16)
-            g.wait_ge(sem(T, NP - 1), arrivals(c, NP - 1, False))
-            k = 16
-            for s in range(len(grp)):
-                if s != me:
-                    g.wait_ge(T.sem.st, k)
-                    g.dma_start(T.y[:], src[:, s * BW:(s + 1) * BW], accum_op=AluOpType.add).then_inc(T.sem.st, 16)
-                    k += 16
-            g.wait_ge(T.sem.st, k)
-        else:
-            g.wait_ge(T.sem.af, 16)
-            g.dma_start(T.y[:], T.fin[:]).then_inc(T.sem.st, 16)
-            g.wait_ge(T.sem.st, 16)
-    g.wait_ge(T.sem.sent, sent)
+        lds = [T.sem.ld0, T.sem.ld1, T.sem.ld2, T.sem.ld3]
+        who = HELP + [3]
+        for i, h in enumerate(who):
+            a = quarter(c, h) * QW
+            g.dma_start(T.xs[:, a:a + QW], T.x[:, a:a + QW]).then_inc(lds[i], 16)
+        sent = 0
+        for i, h in enumerate(who):
+            a = quarter(c, h) * QW
+            g.wait_ge(lds[i], 16)
+            if h != 3:
+                rid, pid = topo.addr(8 * c + h, core)
+                g.remote_dma(T.rq[:], T.xs[:, a:a + QW], T.sem.rl, T.sem.sent, pid, rid, 0xFFFF)
+                sent += 16
+            else:
+                sent += send(g, core, T, topo, T.xs, a, quarter(c, 3))
+        g.wait_ge(T.sem.af, 16)
+        g.dma_start(T.y[:], T.fin[:]).then_inc(T.sem.st, 16)
+        g.wait_ge(T.sem.st, 16)
+        g.wait_ge(T.sem.sent, sent)
+    elif l in HELP:
+        g.wait_ge(T.sem.rl, 16)
+        sent = send(g, core, T, topo, T.rq, 0, quarter(c, l))
+        g.wait_ge(T.sem.sent, sent)
+    elif l == COL:
+        g.wait_ge(T.sem.arr, NR)
+        rid, pid = topo.addr(8 * c + 3, core)
+        g.remote_dma_fused([RemoteDMATransfer(dst_ids=[DstId(rid=rid, pnc=pid)], dma_engine_mask=0xFFFF,
+                                              remote_sem=T.sem.af,
+                                              srcs=[T.land[:, s * BW:(s + 1) * BW] for s in range(NR)],
+                                              dsts=[T.fin[:]], alu_op=1)], local_sem=T.sem.sent)
+        g.wait_ge(T.sem.sent, 16)

@@ -9,8 +9,8 @@ HELP = [7, 6, 2]
 SCRATCH = {
     "xs": ("sbuf", [128, NR * BW], "float32"),
     "rq": ("sbuf", [128, QW], "float32"),
-    "land": ("sbuf", [128, NR * BW], "float32"),
-    "fin": ("sbuf", [128, BW], "float32"),
+    "land": ("dram", [NR, 128, BW], "float32"),
+    "fin": ("dram", [128, BW], "float32"),
 }
 SEMAPHORES = ["ld0", "ld1", "ld2", "ld3", "st", "sent", "rl", "arr", "af"]
 
@@ -26,8 +26,7 @@ def send(g, core, T, topo, src, base, q):
         k = (i + c) % 8
         rid, pid = topo.addr(8 * (8 * q + k) + COL, core)
         trs.append(RemoteDMATransfer(dst_ids=[DstId(rid=rid, pnc=pid)], dma_engine_mask=1 << i, remote_sem=T.sem.arr,
-                                     src=src[:, base + k * BW:base + (k + 1) * BW],
-                                     dst=T.land[:, c * BW:(c + 1) * BW]))
+                                     src=src[:, base + k * BW:base + (k + 1) * BW], dst=T.land[c]))
     g.remote_dma_fused(trs, local_sem=T.sem.sent)
     return 8
 
@@ -62,7 +61,6 @@ def rank_program(g, core, T, topo):
         g.wait_ge(T.sem.arr, NR)
         rid, pid = topo.addr(8 * c + 3, core)
         g.remote_dma_fused([RemoteDMATransfer(dst_ids=[DstId(rid=rid, pnc=pid)], dma_engine_mask=0xFFFF,
-                                              remote_sem=T.sem.af,
-                                              srcs=[T.land[:, s * BW:(s + 1) * BW] for s in range(NR)],
+                                              remote_sem=T.sem.af, srcs=[T.land[s] for s in range(NR)],
                                               dsts=[T.fin[:]], alu_op=1)], local_sem=T.sem.sent)
         g.wait_ge(T.sem.sent, 16)

@@ -2,33 +2,61 @@ from concourse.bass import RemoteDMATransfer, DstId
 
 NR = 32
 BW = 32
-QW = 256
 COL = 1
 HELP = [7, 6, 2]
 
 SCRATCH = {
     "xs": ("sbuf", [128, NR * BW], "float32"),
-    "rq": ("sbuf", [128, QW], "float32"),
+    "rq": ("sbuf", [128, 8 * BW], "float32"),
     "land": ("dram", [NR, 128, BW], "float32"),
     "fin": ("dram", [128, BW], "float32"),
 }
 SEMAPHORES = ["ld0", "ld1", "ld2", "ld3", "st", "sent", "rl", "arr", "af"]
 
 
-def quarter(c, l):
-    return (c >> 3) ^ {3: 0, 2: 1, 7: 2, 6: 3}[l]
+def piece(c, l):
+    q = c >> 3
+    if l == 7:
+        return 8 * (q ^ 2), 8
+    if l == 6:
+        return 8 * (q ^ 3), 8
+    h = 16 * (c >> 4)
+    if q % 2 == 0:
+        return (h, 12) if l == 3 else (h + 12, 4)
+    return (h + 4, 12) if l == 3 else (h, 4)
 
 
-def send(g, core, T, topo, src, base, q):
-    c = core // 8
-    trs = []
-    for i in range(8):
-        k = (i + c) % 8
-        rid, pid = topo.addr(8 * (8 * q + k) + COL, core)
-        trs.append(RemoteDMATransfer(dst_ids=[DstId(rid=rid, pnc=pid)], dma_engine_mask=1 << i, remote_sem=T.sem.arr,
-                                     src=src[:, base + k * BW:base + (k + 1) * BW], dst=T.land[c]))
-    g.remote_dma_fused(trs, local_sem=T.sem.sent)
-    return 8
+def calls(c, l):
+    b, n = piece(c, l)
+    ds = [b + (i + c) % n for i in range(n)]
+    out = []
+    for o in range(0, n, 8):
+        part = ds[o:o + 8]
+        e = 8 // len(part)
+        out.append([(d, ((1 << e) - 1) << (i * e)) for i, d in enumerate(part)])
+    return out
+
+
+def bits(m):
+    return bin(m).count("1")
+
+
+def arrivals(d):
+    return sum(bits(m) for c in range(NR) for l in (3, 2, 7, 6) for call in calls(c, l) for (t, m) in call if t == d)
+
+
+def send(g, core, T, topo, src, first):
+    c, l = core // 8, core % 8
+    n = 0
+    for call in calls(c, l):
+        trs = []
+        for (d, m) in call:
+            rid, pid = topo.addr(8 * d + COL, core)
+            trs.append(RemoteDMATransfer(dst_ids=[DstId(rid=rid, pnc=pid)], dma_engine_mask=m, remote_sem=T.sem.arr,
+                                         src=src[:, (d - first) * BW:(d - first + 1) * BW], dst=T.land[c]))
+            n += bits(m)
+        g.remote_dma_fused(trs, local_sem=T.sem.sent)
+    return n
 
 
 def rank_program(g, core, T, topo):
@@ -37,28 +65,28 @@ def rank_program(g, core, T, topo):
         lds = [T.sem.ld0, T.sem.ld1, T.sem.ld2, T.sem.ld3]
         who = HELP + [3]
         for i, h in enumerate(who):
-            a = quarter(c, h) * QW
-            g.dma_start(T.xs[:, a:a + QW], T.x[:, a:a + QW]).then_inc(lds[i], 16)
+            b, n = piece(c, h)
+            g.dma_start(T.xs[:, b * BW:(b + n) * BW], T.x[:, b * BW:(b + n) * BW]).then_inc(lds[i], 16)
         sent = 0
         for i, h in enumerate(who):
-            a = quarter(c, h) * QW
+            b, n = piece(c, h)
             g.wait_ge(lds[i], 16)
             if h != 3:
                 rid, pid = topo.addr(8 * c + h, core)
-                g.remote_dma(T.rq[:], T.xs[:, a:a + QW], T.sem.rl, T.sem.sent, pid, rid, 0xFFFF)
+                g.remote_dma(T.rq[:, 0:n * BW], T.xs[:, b * BW:(b + n) * BW], T.sem.rl, T.sem.sent, pid, rid, 0xFFFF)
                 sent += 16
             else:
-                sent += send(g, core, T, topo, T.xs, a, quarter(c, 3))
+                sent += send(g, core, T, topo, T.xs, 0)
         g.wait_ge(T.sem.af, 16)
         g.dma_start(T.y[:], T.fin[:]).then_inc(T.sem.st, 16)
         g.wait_ge(T.sem.st, 16)
         g.wait_ge(T.sem.sent, sent)
     elif l in HELP:
         g.wait_ge(T.sem.rl, 16)
-        sent = send(g, core, T, topo, T.rq, 0, quarter(c, l))
+        sent = send(g, core, T, topo, T.rq, piece(c, l)[0])
         g.wait_ge(T.sem.sent, sent)
     elif l == COL:
-        g.wait_ge(T.sem.arr, NR)
+        g.wait_ge(T.sem.arr, arrivals(c))
         rid, pid = topo.addr(8 * c + 3, core)
         g.remote_dma_fused([RemoteDMATransfer(dst_ids=[DstId(rid=rid, pnc=pid)], dma_engine_mask=0xFFFF,
                                               remote_sem=T.sem.af, srcs=[T.land[s] for s in range(NR)],

from concourse.bass import RemoteDMATransfer, DstId

NR = 32
BW = 32
COL = 1
HELP = [7, 6, 2]

SCRATCH = {
    "xs": ("sbuf", [128, NR * BW], "float32"),
    "rq": ("sbuf", [128, 8 * BW], "float32"),
    "land": ("dram", [NR, 128, BW], "float32"),
    "fin": ("dram", [128, BW], "float32"),
}
SEMAPHORES = ["ld0", "ld1", "ld2", "ld3", "st", "sent", "rl", "arr", "af"]


def piece(c, l):
    q = c >> 3
    if l == 7:
        return 8 * (q ^ 2), 8
    if l == 6:
        return 8 * (q ^ 3), 8
    h = 16 * (c >> 4)
    if q % 2 == 0:
        return (h, 12) if l == 3 else (h + 12, 4)
    return (h + 4, 12) if l == 3 else (h, 4)


def calls(c, l):
    b, n = piece(c, l)
    ds = [b + (i + c) % n for i in range(n)]
    out = []
    for o in range(0, n, 8):
        part = ds[o:o + 8]
        e = 8 // len(part)
        out.append([(d, ((1 << e) - 1) << (i * e)) for i, d in enumerate(part)])
    return out


def bits(m):
    return bin(m).count("1")


def arrivals(d):
    return sum(bits(m) for c in range(NR) for l in (3, 2, 7, 6) for call in calls(c, l) for (t, m) in call if t == d)


def send(g, core, T, topo, src, first):
    c, l = core // 8, core % 8
    n = 0
    for call in calls(c, l):
        trs = []
        for (d, m) in call:
            rid, pid = topo.addr(8 * d + COL, core)
            trs.append(RemoteDMATransfer(dst_ids=[DstId(rid=rid, pnc=pid)], dma_engine_mask=m, remote_sem=T.sem.arr,
                                         src=src[:, (d - first) * BW:(d - first + 1) * BW], dst=T.land[c]))
            n += bits(m)
        g.remote_dma_fused(trs, local_sem=T.sem.sent)
    return n


def rank_program(g, core, T, topo):
    c, l = core // 8, core % 8
    if l == 3:
        lds = [T.sem.ld0, T.sem.ld1, T.sem.ld2, T.sem.ld3]
        who = HELP + [3]
        for i, h in enumerate(who):
            b, n = piece(c, h)
            g.dma_start(T.xs[:, b * BW:(b + n) * BW], T.x[:, b * BW:(b + n) * BW]).then_inc(lds[i], 16)
        sent = 0
        for i, h in enumerate(who):
            b, n = piece(c, h)
            g.wait_ge(lds[i], 16)
            if h != 3:
                rid, pid = topo.addr(8 * c + h, core)
                g.remote_dma(T.rq[:, 0:n * BW], T.xs[:, b * BW:(b + n) * BW], T.sem.rl, T.sem.sent, pid, rid, 0xFFFF)
                sent += 16
            else:
                sent += send(g, core, T, topo, T.xs, 0)
        g.wait_ge(T.sem.af, 16)
        g.dma_start(T.y[:], T.fin[:]).then_inc(T.sem.st, 16)
        g.wait_ge(T.sem.st, 16)
        g.wait_ge(T.sem.sent, sent)
    elif l in HELP:
        g.wait_ge(T.sem.rl, 16)
        sent = send(g, core, T, topo, T.rq, piece(c, l)[0])
        g.wait_ge(T.sem.sent, sent)
    elif l == COL:
        g.wait_ge(T.sem.arr, arrivals(c))
        rid, pid = topo.addr(8 * c + 3, core)
        g.remote_dma_fused([RemoteDMATransfer(dst_ids=[DstId(rid=rid, pnc=pid)], dma_engine_mask=0xFFFF,
                                              remote_sem=T.sem.af, srcs=[T.land[s] for s in range(NR)],
                                              dsts=[T.fin[:]], alu_op=1)], local_sem=T.sem.sent)
        g.wait_ge(T.sem.sent, 16)
